import numpy as np
import ml_dtypes


def mxq(x, axis, fmt="e4m3"):
    dtype, down = {"e4m3": (ml_dtypes.float8_e4m3fn, 7), "e5m2": (ml_dtypes.float8_e5m2, 14)}[fmt]
    v = np.moveaxis(np.asarray(x, np.float32).astype(ml_dtypes.bfloat16).astype(np.float64), axis, -1)
    blocks = v.reshape(v.shape[:-1] + (-1, 32))
    amax = np.abs(blocks).max(-1, keepdims=True)
    byte = np.maximum(np.where(amax > 0, np.frexp(amax)[1] - 1 + 127, 0) - down, 1)
    scale = np.exp2(byte - 127.0)
    codes = (blocks / scale).astype(np.float32).astype(dtype).astype(np.float64)
    return np.moveaxis((codes * scale).reshape(v.shape), -1, axis)


WIDE = False


def mx_kscale(k):
    if not WIDE:
        return np.ones(k)
    levels = np.array([10, -10, 5, -5, 0])
    if k % 512:
        return np.exp2(np.random.permutation(np.resize(levels, k // 32))).repeat(32)
    a = np.empty((k // 512, 16))
    for p in range(k // 512):
        a[p, :8] = np.random.permutation(np.resize(levels, 8))
        for g in range(8):
            far = levels[np.abs(levels - a[p, g]) >= 10]
            a[p, g + 8] = far[np.random.randint(len(far))]
    return np.exp2(a.ravel()).repeat(32)


def f64(x):
    return np.asarray(x).astype(np.float64)


def striped(idx):
    return np.tile(np.asarray(idx).reshape(-1, 16).T, (8, 1)).astype(np.uint16)


def unstriped(offs):
    return offs[:16].T.reshape(-1).astype(np.int64)


E2M1 = np.array([0.0, 0.5, 1.0, 1.5, 2.0, 3.0, 4.0, 6.0, -0.0, -0.5, -1.0, -1.5, -2.0, -3.0, -4.0, -6.0])


def pack_weight(w, fmt):
    k, n = w.shape
    w = f64(np.asarray(w, np.float32).astype(ml_dtypes.bfloat16)).reshape(k // 32, 32, n)
    amax = np.abs(w).max(1)
    if fmt == "e4m3":
        byte = np.frexp(amax)[1] - 1 + 127 - 7
    else:
        mant, ex = np.frexp(amax / 6.0)
        byte = np.where(mant > 0.5, ex, ex - 1) + 127
    byte = np.clip(np.where(amax > 0, byte, 1), 1, 254)
    scaled = (w * np.exp2(127.0 - byte)[:, None, :]).reshape(k, n).astype(np.float32)
    by_word = np.ascontiguousarray(scaled.reshape(k // 512, 128, 4, n).transpose(0, 1, 3, 2))
    if fmt == "e4m3":
        words = by_word.astype(ml_dtypes.float8_e4m3fn).view(np.uint8)
    else:
        c = by_word.astype(ml_dtypes.float4_e2m1fn).view(np.uint8) & 0xF
        words = (c[..., 0::2] | (c[..., 1::2] << 4)).reshape(k // 512, 128, 2 * n)
    return np.ascontiguousarray(words), np.ascontiguousarray(byte.astype(np.uint8).reshape(k // 512, 16, n))


def unpack_weight(words, scales, fmt):
    g, _, n = scales.shape
    words = np.ascontiguousarray(words).reshape(g, 128, n, -1)
    if fmt == "e4m3":
        vals = words.view(ml_dtypes.float8_e4m3fn).astype(np.float64)
    else:
        nib = np.empty((g, 128, n, 4), np.uint8)
        nib[..., 0::2] = words & 0xF
        nib[..., 1::2] = words >> 4
        vals = E2M1[nib]
    vals = vals * np.repeat(np.exp2(scales.astype(np.float64) - 127.0), 8, axis=1)[..., None]
    return vals.transpose(0, 1, 3, 2).reshape(g * 512, n)


def softplus(v):
    return np.log(1.0 + np.exp(v))


def sigmoid(v):
    return 1.0 / (1.0 + np.exp(-v))


K, R, F, T, J, M = 512, 128, 512, 2048, 512, 256


def setup_inputs():
    n = np.random.standard_normal
    idx = np.random.permutation(T)[:J]
    idx2 = np.random.permutation(J)[:M]
    idx3 = np.random.permutation(J)[:M]
    fk = mx_kscale(K)
    dtabp = pack_weight(n((K, T)) / fk[:, None], "e2m1")
    tabp = pack_weight(n((K, T)) / fk[:, None], "e2m1")
    return {
        "dtab_words": dtabp[0],
        "dtab_scales": dtabp[1],
        "tab_words": tabp[0],
        "tab_scales": tabp[1],
        "w1": (n((K, R)) * 1 / np.sqrt(K) * fk[:, None]).astype(np.float32),
        "floor": (np.random.uniform(0.2, 0.8, (R, 1))).astype(np.float32),
        "og": (np.random.uniform(0.5, 2.0, (R, 1))).astype(np.float32),
        "base": (0.3 * n((R, M))).astype(np.float32),
        "offs": striped(idx),
        "offs2": striped(idx2),
        "offs3": striped(idx3),
    }


def reference(dtab_words, dtab_scales, tab_words, tab_scales, w1, floor, og, base, offs, offs2, offs3):
    idx = unstriped(offs)
    idx2 = unstriped(offs2)
    idx3 = unstriped(offs3)
    dtabu = unpack_weight(dtab_words, dtab_scales, "e2m1")
    tabu = unpack_weight(tab_words, tab_scales, "e2m1")
    w1q = mxq(f64(w1), 0, "e4m3")
    tabidxg = tabu[:, idx]
    a = w1q.T @ tabidxg
    dtabidxg = dtabu[:, idx]
    ta = w1q.T @ dtabidxg
    h0 = softplus(a)
    h1 = np.log(h0 + f64(floor))
    xh0 = ta * sigmoid(a)
    xh1 = xh0 / (h0 + f64(floor))
    xu1 = (xh1[:, idx2] - xh1[:, idx3]) * sigmoid(h1[:, idx2]) + xh1[:, idx2] * sigmoid(h1[:, idx2]) * (1.0 - sigmoid(h1[:, idx2])) * (h1[:, idx2] - h1[:, idx3])
    y = xu1 * f64(og) + f64(base)
    return y

@@ -1,0 +1,155 @@
+from contextlib import ExitStack
+
+import concourse.mybir as mybir
+
+K, R, T, J, M = 512, 128, 2048, 512, 256
+FLOPS = 2 * 2 * K * R * J
+
+F32 = mybir.dt.float32
+BF16 = mybir.dt.bfloat16
+I32 = mybir.dt.int32
+U32 = mybir.dt.uint32
+U16 = mybir.dt.uint16
+U8 = mybir.dt.uint8
+FP8X4 = mybir.dt.float8_e4m3fn_x4
+FP4X4 = mybir.dt.float4_e2m1fn_x4
+ALU = mybir.AluOpType
+ACT = mybir.ActivationFunctionType
+
+P = 128
+PACK = 4
+HALF = J // 2
+
+
+def load_scale_rows(queues, plane, scales):
+    for quad, queue in enumerate(queues):
+        queue.dma_start(
+            out=plane[32 * quad : 32 * quad + 4, :].bitcast(I32),
+            in_=scales[0, 4 * quad : 4 * quad + 4, :].bitcast(I32),
+        )
+
+
+def tile_attend_tclogratios_kernel(
+    tc, dtab_words, dtab_scales, tab_words, tab_scales, w1, floor, og, base, offs, offs2, offs3, out
+):
+    nc = tc.nc
+    halves = [slice(h * HALF, (h + 1) * HALF) for h in range(2)]
+
+    with ExitStack() as ctx:
+        keep = ctx.enter_context(tc.tile_pool(name="keep", bufs=1))
+        psum = ctx.enter_context(tc.psum_pool(name="psum", bufs=1))
+
+        slots = keep.tile([P, J // 16], U16)
+        firsts = keep.tile([P, M // 16], U16)
+        seconds = keep.tile([P, M // 16], U16)
+        tab_w = keep.tile([P, T], U16, align_bytes=64)
+        tab_s = keep.tile([P, T], U8, align_bytes=64)
+        dtab_w = keep.tile([P, T], U16, align_bytes=64)
+        dtab_s = keep.tile([P, T], U8, tag="dtab_s_then_h0", align_bytes=64)
+        w_raw = keep.tile([P, PACK, R], F32)
+        floor_col = keep.tile([P, 1], F32)
+        og_col = keep.tile([P, 1], F32)
+        base_sb = keep.tile([P, M], F32)
+
+        nc.vector.memset(tab_s[:].bitcast(I32), 0)
+        nc.vector.memset(dtab_s[:].bitcast(I32), 0)
+
+        nc.sync.dma_start(slots[:], offs)
+        nc.sync.dma_start(out=w_raw[:], in_=w1.rearrange("(p j) r -> p j r", j=PACK))
+        load_scale_rows([nc.scalar, nc.scalar, nc.sync, nc.sync], tab_s, tab_scales)
+        nc.sync.dma_start(out=tab_w[:].bitcast(I32), in_=tab_words[0].bitcast(I32))
+        nc.sync.dma_start(out=dtab_w[:].bitcast(I32), in_=dtab_words[0].bitcast(I32))
+        load_scale_rows([nc.sync] * 4, dtab_s, dtab_scales)
+        nc.sync.dma_start(out=floor_col[:], in_=floor)
+        nc.sync.dma_start(firsts[:], offs2)
+        nc.sync.dma_start(seconds[:], offs3)
+        nc.sync.dma_start(out=og_col[:], in_=og)
+        nc.sync.dma_start(out=base_sb[:], in_=base)
+
+        w_grouped = keep.tile([P, R, PACK], BF16, align_bytes=64)
+        nc.scalar.activation(w_grouped[:], w_raw[:].rearrange("p j r -> p r j"), ACT.Copy)
+        w_codes = keep.tile([P, R], U32, align_bytes=64)
+        w_scales = keep.tile([P, R], U8, align_bytes=64)
+
+        tab_gs = keep.tile([P, J], U8, align_bytes=64)
+        nc.vector.tensor_copy(tab_gs[:], tab_s[:].indirect(slots[:]))
+        nc.vector.quantize_mx(
+            out=w_codes[:].bitcast(FP8X4), scales=w_scales[:], in_=w_grouped[:].rearrange("p r j -> p (r j)")
+        )
+
+        a_ps = [psum.tile([P, HALF], F32, name=f"a_ps{h}") for h in range(2)]
+        th = keep.tile([P, J], F32)
+        for h in range(2):
+            tab_gw = keep.tile([P, HALF], U16, name=f"tab_gw{h}", align_bytes=64)
+            nc.vector.tensor_copy(tab_gw[:], tab_w[:].indirect(slots[:, h * HALF // 16 : (h + 1) * HALF // 16]))
+            nc.tensor.matmul_mx(
+                out=a_ps[h][:],
+                lhsT=w_codes[:].bitcast(FP8X4),
+                lhsT_scale=w_scales[:],
+                rhs=tab_gw[:].bitcast(FP4X4),
+                rhs_scale=tab_gs[:, halves[h]],
+                start=True,
+                stop=True,
+            )
+            nc.scalar.activation(th[:, halves[h]], a_ps[h][:], ACT.Tanh, scale=0.5)
+
+        dtab_gw = keep.tile([P, J], U16, align_bytes=64)
+        nc.vector.tensor_copy(dtab_gw[:], dtab_w[:].indirect(slots[:]))
+        th_abs = keep.tile([P, J], F32)
+        for cols in halves:
+            nc.vector.scalar_tensor_tensor(th_abs[:, cols], th[:, cols], -1.0, th[:, cols], ALU.mult, ALU.max)
+        dtab_gs = keep.tile([P, J], U8, align_bytes=64)
+        nc.vector.tensor_copy(dtab_gs[:], dtab_s[:].indirect(slots[:]))
+        ta_ps = psum.tile([P, J], F32)
+        nc.tensor.matmul_mx(
+            out=ta_ps[:],
+            lhsT=w_codes[:].bitcast(FP8X4),
+            lhsT_scale=w_scales[:],
+            rhs=dtab_gw[:].bitcast(FP4X4),
+            rhs_scale=dtab_gs[:],
+            start=True,
+            stop=True,
+        )
+
+        log_sig = keep.tile([P, J], F32)
+        h0 = keep.tile([P, J], F32, tag="dtab_s_then_h0", align_bytes=64)
+        h1 = keep.tile([P, J], F32)
+        for cols in halves:
+            nc.scalar.activation(log_sig[:, cols], th_abs[:, cols], ACT.Ln, bias=0.5, scale=0.5)
+        for h in range(2):
+            cols = halves[h]
+            nc.vector.scalar_tensor_tensor(h0[:, cols], a_ps[h][:], 0.0, log_sig[:, cols], ALU.max, ALU.subtract)
+            nc.scalar.activation(h1[:, cols], h0[:, cols], ACT.Ln, bias=floor_col[:])
+
+        xh0_twice = keep.tile([P, J], F32)
+        nc.vector.scalar_tensor_tensor(xh0_twice[:], th[:], 1.0, ta_ps[:], ALU.add, ALU.mult)
+        h1_first = keep.tile([P, M], F32)
+        nc.vector.tensor_copy(h1_first[:], h1[:].indirect(firsts[:]))
+        h1_gap = keep.tile([P, M], F32)
+        nc.vector.tensor_tensor(h1_gap[:], h1[:].indirect(seconds[:]), h1_first[:], ALU.subtract)
+        gain = keep.tile([P, 1], F32)
+        nc.vector.tensor_scalar(gain[:], og_col[:], -0.5, None, ALU.mult)
+
+        th_first = keep.tile([P, M], F32)
+        nc.scalar.activation(th_first[:], h1_first[:], ACT.Tanh, scale=0.5)
+        inv_u = keep.tile([P, J], F32)
+        for cols in halves:
+            nc.scalar.activation(inv_u[:, cols], h1[:, cols], ACT.Exp, scale=-1.0)
+
+        bend = keep.tile([P, M], F32)
+        nc.vector.scalar_tensor_tensor(bend[:], th_first[:], -1.0, h1_gap[:], ALU.add, ALU.mult)
+        factor = keep.tile([P, M], F32)
+        nc.scalar.activation(factor[:], bend[:], ACT.Identity, bias=1.0, scale=0.5)
+        xh1 = keep.tile([P, J], F32)
+        for cols in halves:
+            nc.vector.scalar_tensor_tensor(xh1[:, cols], inv_u[:, cols], 0.5, xh0_twice[:, cols], ALU.mult, ALU.mult)
+
+        first_term = keep.tile([P, M], F32)
+        nc.vector.tensor_tensor(first_term[:], xh1[:].indirect(firsts[:]), factor[:], ALU.mult)
+        diff = keep.tile([P, M], F32)
+        nc.vector.tensor_tensor(diff[:], xh1[:].indirect(seconds[:]), first_term[:], ALU.subtract)
+        gated = keep.tile([P, M], F32)
+        nc.vector.scalar_tensor_tensor(gated[:], th_first[:], 1.0, diff[:], ALU.add, ALU.mult)
+        result = keep.tile([P, M], F32)
+        nc.vector.scalar_tensor_tensor(result[:], gated[:], gain[:], base_sb[:], ALU.mult, ALU.add)
+        nc.sync.dma_start(out=out, in_=result[:])

@@ -55,30 +55,33 @@ def tile_attend_tclogratios_kernel(
         nc.vector.memset(dtab_s[:].bitcast(I32), 0)
 
         nc.sync.dma_start(slots[:], offs)
-        nc.sync.dma_start(out=w_raw[:], in_=w1.rearrange("(p j) r -> p j r", j=PACK))
-        load_scale_rows([nc.scalar, nc.scalar, nc.sync, nc.sync], tab_s, tab_scales)
+        nc.sync.dma_start(firsts[:], offs2)
+        nc.scalar.dma_start(out=w_raw[:], in_=w1.rearrange("(p j) r -> p j r", j=PACK))
+        load_scale_rows([nc.sync] * 4, tab_s, tab_scales)
         nc.sync.dma_start(out=tab_w[:].bitcast(I32), in_=tab_words[0].bitcast(I32))
         nc.sync.dma_start(out=dtab_w[:].bitcast(I32), in_=dtab_words[0].bitcast(I32))
         load_scale_rows([nc.sync] * 4, dtab_s, dtab_scales)
         nc.sync.dma_start(out=floor_col[:], in_=floor)
-        nc.sync.dma_start(firsts[:], offs2)
         nc.sync.dma_start(seconds[:], offs3)
         nc.sync.dma_start(out=og_col[:], in_=og)
         nc.sync.dma_start(out=base_sb[:], in_=base)
 
         w_grouped = keep.tile([P, R, PACK], BF16, align_bytes=64)
-        nc.scalar.activation(w_grouped[:], w_raw[:].rearrange("p j r -> p r j"), ACT.Copy)
+        w_view = w_raw[:].rearrange("p j r -> p r j")
+        nc.scalar.copy(w_grouped[:, : R // 2, :], w_view[:, : R // 2, :])
+        nc.vector.tensor_copy(w_grouped[:, R // 2 :, :], w_view[:, R // 2 :, :])
         w_codes = keep.tile([P, R], U32, align_bytes=64)
         w_scales = keep.tile([P, R], U8, align_bytes=64)
 
-        tab_gs = keep.tile([P, J], U8, align_bytes=64)
-        nc.vector.tensor_copy(tab_gs[:], tab_s[:].indirect(slots[:]))
         nc.vector.quantize_mx(
             out=w_codes[:].bitcast(FP8X4), scales=w_scales[:], in_=w_grouped[:].rearrange("p r j -> p (r j)")
         )
+        tab_gs = keep.tile([P, J], U8, align_bytes=64)
+        nc.vector.tensor_copy(tab_gs[:], tab_s[:].indirect(slots[:]))
 
         a_ps = [psum.tile([P, HALF], F32, name=f"a_ps{h}") for h in range(2)]
         th = keep.tile([P, J], F32)
+        th_abs0 = keep.tile([P, HALF], F32)
         for h in range(2):
             tab_gw = keep.tile([P, HALF], U16, name=f"tab_gw{h}", align_bytes=64)
             nc.vector.tensor_copy(tab_gw[:], tab_w[:].indirect(slots[:, h * HALF // 16 : (h + 1) * HALF // 16]))
@@ -92,47 +95,51 @@ def tile_attend_tclogratios_kernel(
                 stop=True,
             )
             nc.scalar.activation(th[:, halves[h]], a_ps[h][:], ACT.Tanh, scale=0.5)
+            if h == 0:
+                nc.scalar.activation(th_abs0[:], th[:, halves[0]], ACT.Abs)
 
         dtab_gw = keep.tile([P, J], U16, align_bytes=64)
         nc.vector.tensor_copy(dtab_gw[:], dtab_w[:].indirect(slots[:]))
-        th_abs = keep.tile([P, J], F32)
-        for cols in halves:
-            nc.vector.scalar_tensor_tensor(th_abs[:, cols], th[:, cols], -1.0, th[:, cols], ALU.mult, ALU.max)
-        dtab_gs = keep.tile([P, J], U8, align_bytes=64)
-        nc.vector.tensor_copy(dtab_gs[:], dtab_s[:].indirect(slots[:]))
-        ta_ps = psum.tile([P, J], F32)
-        nc.tensor.matmul_mx(
-            out=ta_ps[:],
-            lhsT=w_codes[:].bitcast(FP8X4),
-            lhsT_scale=w_scales[:],
-            rhs=dtab_gw[:].bitcast(FP4X4),
-            rhs_scale=dtab_gs[:],
-            start=True,
-            stop=True,
-        )
+        ta_ps = [psum.tile([P, HALF], F32, name=f"ta_ps{h}") for h in range(2)]
+        for h in range(2):
+            dtab_gs = keep.tile([P, HALF], U8, name=f"dtab_gs{h}", align_bytes=64)
+            nc.vector.tensor_copy(dtab_gs[:], dtab_s[:].indirect(slots[:, h * HALF // 16 : (h + 1) * HALF // 16]))
+            nc.tensor.matmul_mx(
+                out=ta_ps[h][:],
+                lhsT=w_codes[:].bitcast(FP8X4),
+                lhsT_scale=w_scales[:],
+                rhs=dtab_gw[:, halves[h]].bitcast(FP4X4),
+                rhs_scale=dtab_gs[:],
+                start=True,
+                stop=True,
+            )
+        late = keep.tile([P, J + HALF], F32, tag="dtab_s_then_h0", align_bytes=64)
+        h0, th_abs1 = late[:, :J], late[:, J:]
+        nc.vector.scalar_tensor_tensor(th_abs1, th[:, halves[1]], -1.0, th[:, halves[1]], ALU.mult, ALU.max)
+        xh0_first = keep.tile([P, HALF], F32)
+        nc.vector.scalar_tensor_tensor(xh0_first[:], th[:, halves[0]], 1.0, ta_ps[0][:], ALU.add, ALU.mult)
 
-        log_sig = keep.tile([P, J], F32)
-        h0 = keep.tile([P, J], F32, tag="dtab_s_then_h0", align_bytes=64)
+        log_sig = keep.tile([P, J], F32, tag="log_sig_then_xh0")
         h1 = keep.tile([P, J], F32)
-        for cols in halves:
-            nc.scalar.activation(log_sig[:, cols], th_abs[:, cols], ACT.Ln, bias=0.5, scale=0.5)
+        for cols, th_abs in zip(halves, (th_abs0[:], th_abs1)):
+            nc.scalar.activation(log_sig[:, cols], th_abs, ACT.Ln, bias=0.5, scale=0.5)
         for h in range(2):
             cols = halves[h]
             nc.vector.scalar_tensor_tensor(h0[:, cols], a_ps[h][:], 0.0, log_sig[:, cols], ALU.max, ALU.subtract)
             nc.scalar.activation(h1[:, cols], h0[:, cols], ACT.Ln, bias=floor_col[:])
 
-        xh0_twice = keep.tile([P, J], F32)
-        nc.vector.scalar_tensor_tensor(xh0_twice[:], th[:], 1.0, ta_ps[:], ALU.add, ALU.mult)
-        h1_first = keep.tile([P, M], F32)
+        xh0_second = keep.tile([P, HALF], F32, tag="log_sig_then_xh0")
+        nc.vector.scalar_tensor_tensor(xh0_second[:], th[:, halves[1]], 1.0, ta_ps[1][:], ALU.add, ALU.mult)
+        h1_first = keep.tile([P, M], F32, tag="h1_first_then_inv_u")
         nc.vector.tensor_copy(h1_first[:], h1[:].indirect(firsts[:]))
         h1_gap = keep.tile([P, M], F32)
         nc.vector.tensor_tensor(h1_gap[:], h1[:].indirect(seconds[:]), h1_first[:], ALU.subtract)
-        gain = keep.tile([P, 1], F32)
-        nc.vector.tensor_scalar(gain[:], og_col[:], -0.5, None, ALU.mult)
 
+        gain = keep.tile([P, 1], F32)
+        nc.gpsimd.tensor_scalar(gain[:], og_col[:], -0.5, 0.0, ALU.mult, ALU.add)
         th_first = keep.tile([P, M], F32)
         nc.scalar.activation(th_first[:], h1_first[:], ACT.Tanh, scale=0.5)
-        inv_u = keep.tile([P, J], F32)
+        inv_u = keep.tile([P, J], F32, tag="h1_first_then_inv_u")
         for cols in halves:
             nc.scalar.activation(inv_u[:, cols], h1[:, cols], ACT.Exp, scale=-1.0)
 
@@ -141,15 +148,21 @@ def tile_attend_tclogratios_kernel(
         factor = keep.tile([P, M], F32)
         nc.scalar.activation(factor[:], bend[:], ACT.Identity, bias=1.0, scale=0.5)
         xh1 = keep.tile([P, J], F32)
-        for cols in halves:
-            nc.vector.scalar_tensor_tensor(xh1[:, cols], inv_u[:, cols], 0.5, xh0_twice[:, cols], ALU.mult, ALU.mult)
+        for cols, xh0_twice in zip(halves, (xh0_first, xh0_second)):
+            nc.vector.scalar_tensor_tensor(xh1[:, cols], inv_u[:, cols], 0.5, xh0_twice[:], ALU.mult, ALU.mult)
 
+        pair_halves = [slice(h * M // 2, (h + 1) * M // 2) for h in range(2)]
+        list_halves = [slice(h * M // 32, (h + 1) * M // 32) for h in range(2)]
         first_term = keep.tile([P, M], F32)
-        nc.vector.tensor_tensor(first_term[:], xh1[:].indirect(firsts[:]), factor[:], ALU.mult)
         diff = keep.tile([P, M], F32)
-        nc.vector.tensor_tensor(diff[:], xh1[:].indirect(seconds[:]), first_term[:], ALU.subtract)
         gated = keep.tile([P, M], F32)
-        nc.vector.scalar_tensor_tensor(gated[:], th_first[:], 1.0, diff[:], ALU.add, ALU.mult)
         result = keep.tile([P, M], F32)
-        nc.vector.scalar_tensor_tensor(result[:], gated[:], gain[:], base_sb[:], ALU.mult, ALU.add)
-        nc.sync.dma_start(out=out, in_=result[:])
+        for cols, entries in zip(pair_halves, list_halves):
+            nc.vector.tensor_tensor(first_term[:, cols], xh1[:].indirect(firsts[:, entries]), factor[:, cols], ALU.mult)
+        for cols, entries in zip(pair_halves, list_halves):
+            nc.vector.tensor_tensor(diff[:, cols], xh1[:].indirect(seconds[:, entries]), first_term[:, cols], ALU.subtract)
+        for cols in pair_halves:
+            nc.vector.scalar_tensor_tensor(gated[:, cols], th_first[:, cols], 1.0, diff[:, cols], ALU.add, ALU.mult)
+        for cols, queue in zip(pair_halves, (nc.scalar, nc.sync)):
+            nc.vector.scalar_tensor_tensor(result[:, cols], gated[:, cols], gain[:], base_sb[:, cols], ALU.mult, ALU.add)
+            queue.dma_start(out=out[:, cols], in_=result[:, cols])

from contextlib import ExitStack

import concourse.mybir as mybir

K, R, T, J, M = 512, 128, 2048, 512, 256
FLOPS = 2 * 2 * K * R * J

F32 = mybir.dt.float32
BF16 = mybir.dt.bfloat16
I32 = mybir.dt.int32
U32 = mybir.dt.uint32
U16 = mybir.dt.uint16
U8 = mybir.dt.uint8
FP8X4 = mybir.dt.float8_e4m3fn_x4
FP4X4 = mybir.dt.float4_e2m1fn_x4
ALU = mybir.AluOpType
ACT = mybir.ActivationFunctionType

P = 128
PACK = 4
HALF = J // 2


def load_scale_rows(queues, plane, scales):
    for quad, queue in enumerate(queues):
        queue.dma_start(
            out=plane[32 * quad : 32 * quad + 4, :].bitcast(I32),
            in_=scales[0, 4 * quad : 4 * quad + 4, :].bitcast(I32),
        )


def tile_attend_tclogratios_kernel(
    tc, dtab_words, dtab_scales, tab_words, tab_scales, w1, floor, og, base, offs, offs2, offs3, out
):
    nc = tc.nc
    halves = [slice(h * HALF, (h + 1) * HALF) for h in range(2)]

    with ExitStack() as ctx:
        keep = ctx.enter_context(tc.tile_pool(name="keep", bufs=1))
        psum = ctx.enter_context(tc.psum_pool(name="psum", bufs=1))

        slots = keep.tile([P, J // 16], U16)
        firsts = keep.tile([P, M // 16], U16)
        seconds = keep.tile([P, M // 16], U16)
        tab_w = keep.tile([P, T], U16, align_bytes=64)
        tab_s = keep.tile([P, T], U8, align_bytes=64)
        dtab_w = keep.tile([P, T], U16, align_bytes=64)
        dtab_s = keep.tile([P, T], U8, tag="dtab_s_then_h0", align_bytes=64)
        w_raw = keep.tile([P, PACK, R], F32)
        floor_col = keep.tile([P, 1], F32)
        og_col = keep.tile([P, 1], F32)
        base_sb = keep.tile([P, M], F32)

        nc.vector.memset(tab_s[:].bitcast(I32), 0)
        nc.vector.memset(dtab_s[:].bitcast(I32), 0)

        nc.sync.dma_start(slots[:], offs)
        nc.sync.dma_start(firsts[:], offs2)
        nc.scalar.dma_start(out=w_raw[:], in_=w1.rearrange("(p j) r -> p j r", j=PACK))
        load_scale_rows([nc.sync] * 4, tab_s, tab_scales)
        nc.sync.dma_start(out=tab_w[:].bitcast(I32), in_=tab_words[0].bitcast(I32))
        nc.sync.dma_start(out=dtab_w[:].bitcast(I32), in_=dtab_words[0].bitcast(I32))
        load_scale_rows([nc.sync] * 4, dtab_s, dtab_scales)
        nc.sync.dma_start(out=floor_col[:], in_=floor)
        nc.sync.dma_start(seconds[:], offs3)
        nc.sync.dma_start(out=og_col[:], in_=og)
        nc.sync.dma_start(out=base_sb[:], in_=base)

        w_grouped = keep.tile([P, R, PACK], BF16, align_bytes=64)
        w_view = w_raw[:].rearrange("p j r -> p r j")
        nc.scalar.copy(w_grouped[:, : R // 2, :], w_view[:, : R // 2, :])
        nc.vector.tensor_copy(w_grouped[:, R // 2 :, :], w_view[:, R // 2 :, :])
        w_codes = keep.tile([P, R], U32, align_bytes=64)
        w_scales = keep.tile([P, R], U8, align_bytes=64)

        nc.vector.quantize_mx(
            out=w_codes[:].bitcast(FP8X4), scales=w_scales[:], in_=w_grouped[:].rearrange("p r j -> p (r j)")
        )
        tab_gs = keep.tile([P, J], U8, align_bytes=64)
        nc.vector.tensor_copy(tab_gs[:], tab_s[:].indirect(slots[:]))

        a_ps = [psum.tile([P, HALF], F32, name=f"a_ps{h}") for h in range(2)]
        th = keep.tile([P, J], F32)
        th_abs0 = keep.tile([P, HALF], F32)
        for h in range(2):
            tab_gw = keep.tile([P, HALF], U16, name=f"tab_gw{h}", align_bytes=64)
            nc.vector.tensor_copy(tab_gw[:], tab_w[:].indirect(slots[:, h * HALF // 16 : (h + 1) * HALF // 16]))
            nc.tensor.matmul_mx(
                out=a_ps[h][:],
                lhsT=w_codes[:].bitcast(FP8X4),
                lhsT_scale=w_scales[:],
                rhs=tab_gw[:].bitcast(FP4X4),
                rhs_scale=tab_gs[:, halves[h]],
                start=True,
                stop=True,
            )
            nc.scalar.activation(th[:, halves[h]], a_ps[h][:], ACT.Tanh, scale=0.5)
            if h == 0:
                nc.scalar.activation(th_abs0[:], th[:, halves[0]], ACT.Abs)

        dtab_gw = keep.tile([P, J], U16, align_bytes=64)
        nc.vector.tensor_copy(dtab_gw[:], dtab_w[:].indirect(slots[:]))
        ta_ps = [psum.tile([P, HALF], F32, name=f"ta_ps{h}") for h in range(2)]
        for h in range(2):
            dtab_gs = keep.tile([P, HALF], U8, name=f"dtab_gs{h}", align_bytes=64)
            nc.vector.tensor_copy(dtab_gs[:], dtab_s[:].indirect(slots[:, h * HALF // 16 : (h + 1) * HALF // 16]))
            nc.tensor.matmul_mx(
                out=ta_ps[h][:],
                lhsT=w_codes[:].bitcast(FP8X4),
                lhsT_scale=w_scales[:],
                rhs=dtab_gw[:, halves[h]].bitcast(FP4X4),
                rhs_scale=dtab_gs[:],
                start=True,
                stop=True,
            )
        late = keep.tile([P, J + HALF], F32, tag="dtab_s_then_h0", align_bytes=64)
        h0, th_abs1 = late[:, :J], late[:, J:]
        nc.vector.scalar_tensor_tensor(th_abs1, th[:, halves[1]], -1.0, th[:, halves[1]], ALU.mult, ALU.max)
        xh0_first = keep.tile([P, HALF], F32)
        nc.vector.scalar_tensor_tensor(xh0_first[:], th[:, halves[0]], 1.0, ta_ps[0][:], ALU.add, ALU.mult)

        log_sig = keep.tile([P, J], F32, tag="log_sig_then_xh0")
        h1 = keep.tile([P, J], F32)
        for cols, th_abs in zip(halves, (th_abs0[:], th_abs1)):
            nc.scalar.activation(log_sig[:, cols], th_abs, ACT.Ln, bias=0.5, scale=0.5)
        for h in range(2):
            cols = halves[h]
            nc.vector.scalar_tensor_tensor(h0[:, cols], a_ps[h][:], 0.0, log_sig[:, cols], ALU.max, ALU.subtract)
            nc.scalar.activation(h1[:, cols], h0[:, cols], ACT.Ln, bias=floor_col[:])

        xh0_second = keep.tile([P, HALF], F32, tag="log_sig_then_xh0")
        nc.vector.scalar_tensor_tensor(xh0_second[:], th[:, halves[1]], 1.0, ta_ps[1][:], ALU.add, ALU.mult)
        h1_first = keep.tile([P, M], F32, tag="h1_first_then_inv_u")
        nc.vector.tensor_copy(h1_first[:], h1[:].indirect(firsts[:]))
        h1_gap = keep.tile([P, M], F32)
        nc.vector.tensor_tensor(h1_gap[:], h1[:].indirect(seconds[:]), h1_first[:], ALU.subtract)

        gain = keep.tile([P, 1], F32)
        nc.gpsimd.tensor_scalar(gain[:], og_col[:], -0.5, 0.0, ALU.mult, ALU.add)
        th_first = keep.tile([P, M], F32)
        nc.scalar.activation(th_first[:], h1_first[:], ACT.Tanh, scale=0.5)
        inv_u = keep.tile([P, J], F32, tag="h1_first_then_inv_u")
        for cols in halves:
            nc.scalar.activation(inv_u[:, cols], h1[:, cols], ACT.Exp, scale=-1.0)

        bend = keep.tile([P, M], F32)
        nc.vector.scalar_tensor_tensor(bend[:], th_first[:], -1.0, h1_gap[:], ALU.add, ALU.mult)
        factor = keep.tile([P, M], F32)
        nc.scalar.activation(factor[:], bend[:], ACT.Identity, bias=1.0, scale=0.5)
        xh1 = keep.tile([P, J], F32)
        for cols, xh0_twice in zip(halves, (xh0_first, xh0_second)):
            nc.vector.scalar_tensor_tensor(xh1[:, cols], inv_u[:, cols], 0.5, xh0_twice[:], ALU.mult, ALU.mult)

        pair_halves = [slice(h * M // 2, (h + 1) * M // 2) for h in range(2)]
        list_halves = [slice(h * M // 32, (h + 1) * M // 32) for h in range(2)]
        first_term = keep.tile([P, M], F32)
        diff = keep.tile([P, M], F32)
        gated = keep.tile([P, M], F32)
        result = keep.tile([P, M], F32)
        for cols, entries in zip(pair_halves, list_halves):
            nc.vector.tensor_tensor(first_term[:, cols], xh1[:].indirect(firsts[:, entries]), factor[:, cols], ALU.mult)
        for cols, entries in zip(pair_halves, list_halves):
            nc.vector.tensor_tensor(diff[:, cols], xh1[:].indirect(seconds[:, entries]), first_term[:, cols], ALU.subtract)
        for cols in pair_halves:
            nc.vector.scalar_tensor_tensor(gated[:, cols], th_first[:, cols], 1.0, diff[:, cols], ALU.add, ALU.mult)
        for cols, queue in zip(pair_halves, (nc.scalar, nc.sync)):
            nc.vector.scalar_tensor_tensor(result[:, cols], gated[:, cols], gain[:], base_sb[:, cols], ALU.mult, ALU.add)
            queue.dma_start(out=out[:, cols], in_=result[:, cols])
